import numpy as np
import ml_dtypes


def mxq(x, axis, fmt="e4m3"):
    dtype, down = {"e4m3": (ml_dtypes.float8_e4m3fn, 7), "e5m2": (ml_dtypes.float8_e5m2, 14)}[fmt]
    v = np.moveaxis(np.asarray(x, np.float32).astype(ml_dtypes.bfloat16).astype(np.float64), axis, -1)
    blocks = v.reshape(v.shape[:-1] + (-1, 32))
    amax = np.abs(blocks).max(-1, keepdims=True)
    byte = np.maximum(np.where(amax > 0, np.frexp(amax)[1] - 1 + 127, 0) - down, 1)
    scale = np.exp2(byte - 127.0)
    codes = (blocks / scale).astype(np.float32).astype(dtype).astype(np.float64)
    return np.moveaxis((codes * scale).reshape(v.shape), -1, axis)


WIDE = False


def mx_kscale(k):
    if not WIDE:
        return np.ones(k)
    levels = np.array([10, -10, 5, -5, 0])
    if k % 512:
        return np.exp2(np.random.permutation(np.resize(levels, k // 32))).repeat(32)
    a = np.empty((k // 512, 16))
    for p in range(k // 512):
        a[p, :8] = np.random.permutation(np.resize(levels, 8))
        for g in range(8):
            far = levels[np.abs(levels - a[p, g]) >= 10]
            a[p, g + 8] = far[np.random.randint(len(far))]
    return np.exp2(a.ravel()).repeat(32)


def f64(x):
    return np.asarray(x).astype(np.float64)


def striped(idx):
    return np.tile(np.asarray(idx).reshape(-1, 16).T, (8, 1)).astype(np.uint16)


def unstriped(offs):
    return offs[:16].T.reshape(-1).astype(np.int64)


E2M1 = np.array([0.0, 0.5, 1.0, 1.5, 2.0, 3.0, 4.0, 6.0, -0.0, -0.5, -1.0, -1.5, -2.0, -3.0, -4.0, -6.0])


def pack_weight(w, fmt):
    k, n = w.shape
    w = f64(np.asarray(w, np.float32).astype(ml_dtypes.bfloat16)).reshape(k // 32, 32, n)
    amax = np.abs(w).max(1)
    if fmt == "e4m3":
        byte = np.frexp(amax)[1] - 1 + 127 - 7
    else:
        mant, ex = np.frexp(amax / 6.0)
        byte = np.where(mant > 0.5, ex, ex - 1) + 127
    byte = np.clip(np.where(amax > 0, byte, 1), 1, 254)
    scaled = (w * np.exp2(127.0 - byte)[:, None, :]).reshape(k, n).astype(np.float32)
    by_word = np.ascontiguousarray(scaled.reshape(k // 512, 128, 4, n).transpose(0, 1, 3, 2))
    if fmt == "e4m3":
        words = by_word.astype(ml_dtypes.float8_e4m3fn).view(np.uint8)
    else:
        c = by_word.astype(ml_dtypes.float4_e2m1fn).view(np.uint8) & 0xF
        words = (c[..., 0::2] | (c[..., 1::2] << 4)).reshape(k // 512, 128, 2 * n)
    return np.ascontiguousarray(words), np.ascontiguousarray(byte.astype(np.uint8).reshape(k // 512, 16, n))


def unpack_weight(words, scales, fmt):
    g, _, n = scales.shape
    words = np.ascontiguousarray(words).reshape(g, 128, n, -1)
    if fmt == "e4m3":
        vals = words.view(ml_dtypes.float8_e4m3fn).astype(np.float64)
    else:
        nib = np.empty((g, 128, n, 4), np.uint8)
        nib[..., 0::2] = words & 0xF
        nib[..., 1::2] = words >> 4
        vals = E2M1[nib]
    vals = vals * np.repeat(np.exp2(scales.astype(np.float64) - 127.0), 8, axis=1)[..., None]
    return vals.transpose(0, 1, 3, 2).reshape(g * 512, n)


def bf(x):
    return np.asarray(x, np.float32).astype(ml_dtypes.bfloat16)


def planes(Y):
    r, m = Y.shape
    b = f64(bf(Y)).reshape(r // 32, 32, m)
    amax = np.abs(b).max(1)
    byte = np.clip(np.where(amax > 0, np.frexp(amax)[1] - 1 + 127 - 7, 1), 1, 254)
    codes = (b * np.exp2(127.0 - byte)[:, None, :]).reshape(r, m).astype(np.float32).astype(ml_dtypes.float8_e4m3fn).view(np.uint8)
    words = codes.reshape(r // 512, 128, 4, m).transpose(0, 1, 3, 2)
    return np.ascontiguousarray(words), np.ascontiguousarray(byte.astype(np.uint8).reshape(r // 512, 16, m))


K, T, J, N = 1024, 2048, 512, 512


def setup_inputs():
    n = np.random.standard_normal
    idx = np.random.permutation(T)[:J]
    idx2 = np.random.permutation(T)[:J]
    fk = mx_kscale(K)
    wap = pack_weight(n((K, N)) * 1 / np.sqrt(K) * fk[:, None], "e2m1")
    wbp = pack_weight(n((K, N)) * 1 / np.sqrt(K) * fk[:, None], "e4m3")
    return {
        "xt": (n((K, T)) * np.random.uniform(0.3, 1.7, (1, T)) / fk[:, None]).astype(np.float32),
        "wa_words": wap[0],
        "wa_scales": wap[1],
        "wb_words": wbp[0],
        "wb_scales": wbp[1],
        "offs": striped(idx),
        "offs2": striped(idx2),
    }


def reference(xt, wa_words, wa_scales, wb_words, wb_scales, offs, offs2):
    idx = unstriped(offs)
    idx2 = unstriped(offs2)
    wau = unpack_weight(wa_words, wa_scales, "e2m1")
    wbu = unpack_weight(wb_words, wb_scales, "e4m3")
    xtidxq = mxq(f64(xt)[:, idx], 0, "e4m3")
    a = xtidxq.T @ wau
    xtidx2q = mxq(f64(xt)[:, idx2], 0, "e4m3")
    b = xtidx2q.T @ wbu
    sa = np.sqrt(np.mean(np.square(a), axis=1, keepdims=True) + 0.01)
    sb = np.sqrt(np.mean(np.square(b), axis=1, keepdims=True) + 0.01)
    y = a * sb / sa + 0.3 * b
    words, scales = planes(y)
    return y, words, scales

@@ -1,0 +1,231 @@
+from contextlib import ExitStack
+
+import concourse.mybir as mybir
+
+K, T, J, N = 1024, 2048, 512, 512
+FLOPS = 2 * 2 * J * K * N
+
+F32 = mybir.dt.float32
+BF16 = mybir.dt.bfloat16
+I32 = mybir.dt.int32
+U32 = mybir.dt.uint32
+U16 = mybir.dt.uint16
+U8 = mybir.dt.uint8
+FP8X4 = mybir.dt.float8_e4m3fn_x4
+FP4X4 = mybir.dt.float4_e2m1fn_x4
+ACT = mybir.ActivationFunctionType
+ALU = mybir.AluOpType
+
+P = 128
+PASSES = 2
+EPS_SUM = 0.01 * N
+CHUNKS = ((1024, 1024), (1024, 768, 256), (1024, 768, 256), (768, 768, 256, 256))
+VECTOR_SHARE = ((640, 640), (0, 768, 0), (0, 768, 0), (0, 256, 128, 192))
+
+
+def tile_moe_expert_sized_like_other_pl_kernel(
+    tc, xt, wa_words, wa_scales, wb_words, wb_scales, offs, offs2, out_0, out_1, out_2
+):
+    nc = tc.nc
+    with ExitStack() as ctx:
+        keep = ctx.enter_context(tc.tile_pool(name="keep", bufs=1))
+        psum = ctx.enter_context(tc.psum_pool(name="psum", bufs=1))
+
+        list_a = keep.tile([P, J // 16], U16, name="list_a")
+        list_b = keep.tile([P, J // 16], U16, name="list_b")
+
+        warm = keep.tile([P, 1], F32, name="warm")
+        warm_out = keep.tile([P, 1], F32, name="warm_out")
+        nc.vector.memset(warm[:], 1.0)
+        nc.scalar.activation(warm_out[:], warm[:], ACT.Abs_reciprocal_sqrt)
+
+        wa_plane = keep.tile([P, PASSES, N], U8, name="wa_plane", align_bytes=64)
+        wb_plane = keep.tile([P, PASSES, N], U8, name="wb_plane", align_bytes=64)
+        nc.gpsimd.memset(wb_plane[:].bitcast(I32), 0)
+        nc.gpsimd.memset(wa_plane[:].bitcast(I32), 0)
+
+        x_rows = xt.rearrange("(g p u e) t -> g u p e t", g=PASSES, u=2, e=2)
+        raw = {}
+
+        def load_x(pair, c):
+            c0 = sum(CHUNKS[pair][:c])
+            width = CHUNKS[pair][c]
+            raw[pair, c] = keep.tile([P, 2, width], F32, name="raw_%d_%d" % (pair, c))
+            nc.sync.dma_start(raw[pair, c][:], x_rows[pair // 2, pair % 2, :, :, c0 : c0 + width])
+
+        def load_plane(plane, scales):
+            rows = scales.rearrange("g (q r) n -> r q g n", r=4)
+            for r in range(4):
+                nc.sync.dma_start(plane[:].bitcast(I32)[r:P:32], rows[r].bitcast(I32))
+
+        wb_sb = [keep.tile([P, 4 * N], U8, name="wb_sb%d" % g, align_bytes=64) for g in range(PASSES)]
+        wa_sb = keep.tile([P, PASSES, 2 * N], U8, name="wa_sb", align_bytes=64)
+        load_x(0, 0)
+        nc.sync.dma_start(list_a[:], offs)
+        nc.sync.dma_start(list_b[:], offs2)
+        load_x(0, 1)
+        for pair in (1, 2):
+            for c in range(3):
+                load_x(pair, c)
+        load_x(3, 0)
+        load_plane(wb_plane, wb_scales)
+        for c in (1, 2, 3):
+            load_x(3, c)
+        for g in range(PASSES):
+            nc.sync.dma_start(wb_sb[g][:].bitcast(I32), wb_words[g].rearrange("p n t -> p (n t)").bitcast(I32))
+        nc.sync.dma_start(wa_sb[:].bitcast(I32), wa_words.rearrange("g p n -> p g n").bitcast(I32))
+        load_plane(wa_plane, wa_scales)
+
+        pairs = [keep.tile([P, 2 * T], BF16, name="pairs%d" % i, align_bytes=64) for i in range(4)]
+
+        def cast(pair):
+            c0 = 0
+            dst = pairs[pair][:].rearrange("p (t e) -> p t e", e=2)
+            for c, width in enumerate(CHUNKS[pair]):
+                src = raw[pair, c][:].rearrange("p e t -> p t e")
+                v = VECTOR_SHARE[pair][c]
+                if v < width:
+                    nc.scalar.activation(dst[:, c0 + v : c0 + width, :], src[:, v:width, :], ACT.Copy)
+                if v > 0:
+                    nc.vector.tensor_copy(dst[:, c0 : c0 + v, :], src[:, 0:v, :])
+                c0 += width
+
+        lists = {"a": list_a, "b": list_b}
+        picked = {}
+        grouped = {}
+        codes = {}
+        plane = {}
+        for s in "ba":
+            for g in range(PASSES):
+                grouped[s, g] = keep.tile([P, 4 * J], BF16, name="grouped_%s%d" % (s, g), align_bytes=64)
+                codes[s, g] = keep.tile([P, J], U32, name="codes_%s%d" % (s, g), align_bytes=64)
+                plane[s, g] = keep.tile([P, J], U8, name="plane_%s%d" % (s, g), align_bytes=64)
+        for key in (("b", 0), ("a", 0), ("a", 1)):
+            picked[key] = keep.tile([P, 2, J], U32, name="picked_%s%d" % key)
+
+        def gather_plain(s, pair):
+            window = pairs[pair][:].bitcast(U32)
+            nc.vector.tensor_copy(picked[s, pair // 2][:, pair % 2, :], window.indirect(lists[s][:]))
+
+        def gather_in_place(s, pair):
+            window = pairs[pair][:].bitcast(U32)
+            dst = grouped[s, pair // 2][:].bitcast(U32).rearrange("p (t m u) -> p u m t", t=4, u=2)
+            nc.vector.tensor_copy(dst[:, pair % 2, :, :], window.indirect(lists[s][:]))
+
+        def weave(s, g, on_vector):
+            dt = I32 if on_vector else U32
+            dst = grouped[s, g][:].bitcast(dt).rearrange("p (t m u) -> p m u t", t=4, u=2)
+            src = picked[s, g][:].bitcast(dt).rearrange("p u (m t) -> p m u t", t=4)
+            if on_vector:
+                nc.vector.tensor_copy(dst, src)
+            else:
+                nc.scalar.copy(dst, src)
+
+        def quantise(s, g, pieces):
+            w = J // pieces
+            for i in range(pieces):
+                nc.vector.quantize_mx(
+                    out=codes[s, g][:, i * w : (i + 1) * w].bitcast(FP8X4),
+                    scales=plane[s, g][:, i * w : (i + 1) * w],
+                    in_=grouped[s, g][:, 4 * i * w : 4 * (i + 1) * w],
+                )
+
+        bank = {}
+        for s in "ba":
+            for t in range(4):
+                bank[s, t] = psum.tile([P, N], F32, name="bank_%s%d" % (s, t))
+
+        def multiply(s, g, slices=range(4)):
+            for t in slices:
+                cols = slice(t * P, (t + 1) * P)
+                if s == "a":
+                    w, ws = wa_sb[:, g, :].bitcast(FP4X4), wa_plane[:, g, :]
+                else:
+                    w, ws = wb_sb[g][:].bitcast(FP8X4), wb_plane[:, g, :]
+                nc.tensor.matmul_mx(
+                    out=bank[s, t][:],
+                    lhsT=codes[s, g][:, cols].bitcast(FP8X4),
+                    lhsT_scale=plane[s, g][:, cols],
+                    rhs=w,
+                    rhs_scale=ws,
+                    start=(g == 0),
+                    stop=(g == PASSES - 1),
+                )
+
+        cast(0)
+        gather_plain("b", 0)
+        gather_plain("a", 0)
+        cast(1)
+        gather_plain("b", 1)
+        gather_plain("a", 1)
+        weave("b", 0, False)
+        weave("a", 0, True)
+        quantise("b", 0, 1)
+        quantise("a", 0, 1)
+        cast(2)
+        gather_plain("a", 2)
+        gather_in_place("b", 2)
+        cast(3)
+        gather_plain("a", 3)
+        gather_in_place("b", 3)
+        weave("a", 1, False)
+        multiply("b", 0)
+        quantise("b", 1, 4)
+        multiply("b", 1)
+        quantise("a", 1, 4)
+        for t in range(4):
+            multiply("a", 0, (t,))
+            multiply("a", 1, (t,))
+
+        squares = keep.tile([P, N], BF16, name="squares")
+        sum_a = keep.tile([P, 4], F32, name="sum_a")
+        sum_b = keep.tile([P, 4], F32, name="sum_b")
+        denom = keep.tile([P, 8], F32, name="denom")
+        recip = keep.tile([P, 8], F32, name="recip")
+        factor = keep.tile([P, 4], F32, name="factor")
+        part_b = keep.tile([P, 4, N], F32, name="part_b")
+        y = keep.tile([P, 4, N], F32, name="y")
+        for t in range(4):
+            nc.scalar.activation(squares[:], bank["b", t][:], ACT.Square, accum_out=sum_b[:, t : t + 1])
+            if t < 3:
+                nc.vector.tensor_scalar(part_b[:, t, :], bank["b", t][:], 0.3, None, ALU.mult)
+        nc.vector.tensor_scalar(denom[:, 0:4], sum_b[:], EPS_SUM, None, ALU.add)
+        nc.vector.tensor_scalar(denom[:, 4:8], sum_b[:], 1.0 / EPS_SUM, 1.0, ALU.mult, ALU.add)
+        nc.vector.reciprocal(recip[:], denom[:])
+        nc.vector.tensor_scalar(part_b[:, 3, :], bank["b", 3][:], 0.3, None, ALU.mult)
+        out_rows = out_0.rearrange("(p t) n -> p t n", t=4)
+        for t in range(4):
+            nc.scalar.activation(squares[:], bank["a", t][:], ACT.Square, accum_out=sum_a[:, t : t + 1])
+            nc.scalar.activation(
+                factor[:, t : t + 1],
+                sum_a[:, t : t + 1],
+                ACT.Abs_reciprocal_sqrt,
+                bias=recip[:, 4 + t : 5 + t],
+                scale=recip[:, t : t + 1],
+            )
+            nc.vector.scalar_tensor_tensor(
+                y[:, t, :], bank["a", t][:], factor[:, t : t + 1], part_b[:, t, :], ALU.mult, ALU.add
+            )
+            nc.sync.dma_start(out_rows[:, t, :], y[:, t, :])
+
+        y_grouped = keep.tile([P, 4 * N], BF16, name="y_grouped", align_bytes=64)
+        y_codes = keep.tile([P, N], U32, name="y_codes", align_bytes=64)
+        y_plane = keep.tile([P, N], U8, name="y_plane", align_bytes=64)
+        half = N // 2
+        dst = y_grouped[:].rearrange("p (c i t) -> p c t i", i=4, t=4)
+        src = y[:].rearrange("p t (c i) -> p c t i", i=4)
+        nc.scalar.activation(dst[:, half // 4 :], src[:, half // 4 :], ACT.Copy)
+        nc.vector.tensor_copy(dst[:, : half // 4], src[:, : half // 4])
+        words_out = out_1[0].rearrange("p n t -> p (n t)").bitcast(I32)
+        for h, queue in ((0, nc.sync), (1, nc.scalar)):
+            cols = slice(h * half, (h + 1) * half)
+            nc.vector.quantize_mx(
+                out=y_codes[:, cols].bitcast(FP8X4),
+                scales=y_plane[:, cols],
+                in_=y_grouped[:, 4 * h * half : 4 * (h + 1) * half],
+            )
+            queue.dma_start(words_out[:, cols], y_codes[:, cols].bitcast(I32))
+        scale_rows = out_2[0].rearrange("(q r) n -> r q n", r=4)
+        for r in range(4):
+            queue = nc.sync if r % 2 == 0 else nc.scalar
+            queue.dma_start(scale_rows[r].bitcast(I32), y_plane[:].bitcast(I32)[r:P:32])

@@ -18,7 +18,7 @@ ALU = mybir.AluOpType
 
 P = 128
 PASSES = 2
-EPS_SUM = 0.01 * N
+UNIT = (0.01 * N) ** -0.5
 CHUNKS = ((1024, 1024), (1024, 768, 256), (1024, 768, 256), (768, 768, 256, 256))
 VECTOR_SHARE = ((640, 640), (0, 768, 0), (0, 768, 0), (0, 256, 128, 192))
 
@@ -67,10 +67,9 @@ def tile_moe_expert_sized_like_other_pl_kernel(
         for pair in (1, 2):
             for c in range(3):
                 load_x(pair, c)
-        load_x(3, 0)
-        load_plane(wb_plane, wb_scales)
-        for c in (1, 2, 3):
+        for c in range(4):
             load_x(3, c)
+        load_plane(wb_plane, wb_scales)
         for g in range(PASSES):
             nc.sync.dma_start(wb_sb[g][:].bitcast(I32), wb_words[g].rearrange("p n t -> p (n t)").bitcast(I32))
         nc.sync.dma_start(wa_sb[:].bitcast(I32), wa_words.rearrange("g p n -> p g n").bitcast(I32))
@@ -100,22 +99,17 @@ def tile_moe_expert_sized_like_other_pl_kernel(
                 grouped[s, g] = keep.tile([P, 4 * J], BF16, name="grouped_%s%d" % (s, g), align_bytes=64)
                 codes[s, g] = keep.tile([P, J], U32, name="codes_%s%d" % (s, g), align_bytes=64)
                 plane[s, g] = keep.tile([P, J], U8, name="plane_%s%d" % (s, g), align_bytes=64)
-        for key in (("b", 0), ("a", 0), ("a", 1)):
+        for key in (("b", 0), ("a", 0), ("b", 1), ("a", 1)):
             picked[key] = keep.tile([P, 2, J], U32, name="picked_%s%d" % key)
 
         def gather_plain(s, pair):
             window = pairs[pair][:].bitcast(U32)
             nc.vector.tensor_copy(picked[s, pair // 2][:, pair % 2, :], window.indirect(lists[s][:]))
 
-        def gather_in_place(s, pair):
-            window = pairs[pair][:].bitcast(U32)
-            dst = grouped[s, pair // 2][:].bitcast(U32).rearrange("p (t m u) -> p u m t", t=4, u=2)
-            nc.vector.tensor_copy(dst[:, pair % 2, :, :], window.indirect(lists[s][:]))
-
-        def weave(s, g, on_vector):
+        def weave(s, g, on_vector, m0=0, m1=P):
             dt = I32 if on_vector else U32
-            dst = grouped[s, g][:].bitcast(dt).rearrange("p (t m u) -> p m u t", t=4, u=2)
-            src = picked[s, g][:].bitcast(dt).rearrange("p u (m t) -> p m u t", t=4)
+            dst = grouped[s, g][:].bitcast(dt).rearrange("p (t m u) -> p m u t", t=4, u=2)[:, m0:m1]
+            src = picked[s, g][:].bitcast(dt).rearrange("p u (m t) -> p m u t", t=4)[:, m0:m1]
             if on_vector:
                 nc.vector.tensor_copy(dst, src)
             else:
@@ -163,14 +157,16 @@ def tile_moe_expert_sized_like_other_pl_kernel(
         quantise("b", 0, 1)
         quantise("a", 0, 1)
         cast(2)
+        gather_plain("b", 2)
         gather_plain("a", 2)
-        gather_in_place("b", 2)
         cast(3)
+        gather_plain("b", 3)
         gather_plain("a", 3)
-        gather_in_place("b", 3)
-        weave("a", 1, False)
+        weave("b", 1, False)
+        weave("a", 1, False, 0, 64)
         multiply("b", 0)
         quantise("b", 1, 4)
+        weave("a", 1, True, 64, P)
         multiply("b", 1)
         quantise("a", 1, 4)
         for t in range(4):
@@ -180,27 +176,24 @@ def tile_moe_expert_sized_like_other_pl_kernel(
         squares = keep.tile([P, N], BF16, name="squares")
         sum_a = keep.tile([P, 4], F32, name="sum_a")
         sum_b = keep.tile([P, 4], F32, name="sum_b")
-        denom = keep.tile([P, 8], F32, name="denom")
-        recip = keep.tile([P, 8], F32, name="recip")
+        denom = keep.tile([P, 4], F32, name="denom")
+        recip = keep.tile([P, 4], F32, name="recip")
         factor = keep.tile([P, 4], F32, name="factor")
         part_b = keep.tile([P, 4, N], F32, name="part_b")
         y = keep.tile([P, 4, N], F32, name="y")
         for t in range(4):
-            nc.scalar.activation(squares[:], bank["b", t][:], ACT.Square, accum_out=sum_b[:, t : t + 1])
-            if t < 3:
-                nc.vector.tensor_scalar(part_b[:, t, :], bank["b", t][:], 0.3, None, ALU.mult)
-        nc.vector.tensor_scalar(denom[:, 0:4], sum_b[:], EPS_SUM, None, ALU.add)
-        nc.vector.tensor_scalar(denom[:, 4:8], sum_b[:], 1.0 / EPS_SUM, 1.0, ALU.mult, ALU.add)
-        nc.vector.reciprocal(recip[:], denom[:])
-        nc.vector.tensor_scalar(part_b[:, 3, :], bank["b", 3][:], 0.3, None, ALU.mult)
+            nc.scalar.activation(squares[:], bank["b", t][:], ACT.Square, scale=UNIT, accum_out=sum_b[:, t : t + 1])
+            nc.vector.tensor_scalar(part_b[:, t, :], bank["b", t][:], 0.3, None, ALU.mult)
+        nc.scalar.activation(denom[:], sum_b[:], ACT.Abs_reciprocal_sqrt, bias=warm[:])
+        nc.scalar.activation(recip[:], denom[:], ACT.Square)
         out_rows = out_0.rearrange("(p t) n -> p t n", t=4)
         for t in range(4):
-            nc.scalar.activation(squares[:], bank["a", t][:], ACT.Square, accum_out=sum_a[:, t : t + 1])
+            nc.scalar.activation(squares[:], bank["a", t][:], ACT.Square, scale=UNIT, accum_out=sum_a[:, t : t + 1])
             nc.scalar.activation(
                 factor[:, t : t + 1],
                 sum_a[:, t : t + 1],
                 ACT.Abs_reciprocal_sqrt,
-                bias=recip[:, 4 + t : 5 + t],
+                bias=recip[:, t : t + 1],
                 scale=recip[:, t : t + 1],
             )
             nc.vector.scalar_tensor_tensor(
@@ -214,8 +207,9 @@ def tile_moe_expert_sized_like_other_pl_kernel(
         half = N // 2
         dst = y_grouped[:].rearrange("p (c i t) -> p c t i", i=4, t=4)
         src = y[:].rearrange("p t (c i) -> p c t i", i=4)
-        nc.scalar.activation(dst[:, half // 4 :], src[:, half // 4 :], ACT.Copy)
-        nc.vector.tensor_copy(dst[:, : half // 4], src[:, : half // 4])
+        split = 320 // 4
+        nc.scalar.activation(dst[:, split:], src[:, split:], ACT.Copy)
+        nc.vector.tensor_copy(dst[:, :split], src[:, :split])
         words_out = out_1[0].rearrange("p n t -> p (n t)").bitcast(I32)
         for h, queue in ((0, nc.sync), (1, nc.scalar)):
             cols = slice(h * half, (h + 1) * half)

@@ -19,8 +19,8 @@ ALU = mybir.AluOpType
 P = 128
 PASSES = 2
 UNIT = (0.01 * N) ** -0.5
-CHUNKS = ((1024, 1024), (1024, 768, 256), (1024, 768, 256), (768, 768, 256, 256))
-VECTOR_SHARE = ((640, 640), (0, 768, 0), (0, 768, 0), (0, 256, 128, 192))
+CHUNKS = ((1024, 1024), (1024, 1024), (1024, 1024), (768, 768, 512))
+VECTOR_SHARE = ((688, 688), (0, 688), (0, 256), (0, 192, 344))
 
 
 def tile_moe_expert_sized_like_other_pl_kernel(
@@ -48,9 +48,9 @@ def tile_moe_expert_sized_like_other_pl_kernel(
         raw = {}
 
         def load_x(pair, c):
-            c0 = sum(CHUNKS[pair][:c])
             width = CHUNKS[pair][c]
-            raw[pair, c] = keep.tile([P, 2, width], F32, name="raw_%d_%d" % (pair, c))
+            c0 = T - sum(CHUNKS[pair][: c + 1])
+            raw[pair, c] = keep.tile([P, 2, width], F32, name="raw_%d_%d" % (pair, c), tag="raw_%d_%d" % (pair, c), align_bytes=64)
             nc.sync.dma_start(raw[pair, c][:], x_rows[pair // 2, pair % 2, :, :, c0 : c0 + width])
 
         def load_plane(plane, scales):
@@ -59,35 +59,33 @@ def tile_moe_expert_sized_like_other_pl_kernel(
                 nc.sync.dma_start(plane[:].bitcast(I32)[r:P:32], rows[r].bitcast(I32))
 
         wb_sb = [keep.tile([P, 4 * N], U8, name="wb_sb%d" % g, align_bytes=64) for g in range(PASSES)]
-        wa_sb = keep.tile([P, PASSES, 2 * N], U8, name="wa_sb", align_bytes=64)
         load_x(0, 0)
         nc.sync.dma_start(list_a[:], offs)
         nc.sync.dma_start(list_b[:], offs2)
         load_x(0, 1)
         for pair in (1, 2):
-            for c in range(3):
+            for c in range(2):
                 load_x(pair, c)
-        for c in range(4):
+        for c in range(3):
             load_x(3, c)
         load_plane(wb_plane, wb_scales)
         for g in range(PASSES):
             nc.sync.dma_start(wb_sb[g][:].bitcast(I32), wb_words[g].rearrange("p n t -> p (n t)").bitcast(I32))
-        nc.sync.dma_start(wa_sb[:].bitcast(I32), wa_words.rearrange("g p n -> p g n").bitcast(I32))
         load_plane(wa_plane, wa_scales)
 
-        pairs = [keep.tile([P, 2 * T], BF16, name="pairs%d" % i, align_bytes=64) for i in range(4)]
+        pair_tiles = [keep.tile([P, 2 * T], BF16, name="pairs%d" % i, align_bytes=64) for i in range(4)]
+        pairs = [tile[:] for tile in pair_tiles]
 
         def cast(pair):
-            c0 = 0
-            dst = pairs[pair][:].rearrange("p (t e) -> p t e", e=2)
+            dst = pairs[pair].rearrange("p (t e) -> p t e", e=2)
             for c, width in enumerate(CHUNKS[pair]):
+                c0 = T - sum(CHUNKS[pair][: c + 1])
                 src = raw[pair, c][:].rearrange("p e t -> p t e")
                 v = VECTOR_SHARE[pair][c]
                 if v < width:
                     nc.scalar.activation(dst[:, c0 + v : c0 + width, :], src[:, v:width, :], ACT.Copy)
                 if v > 0:
                     nc.vector.tensor_copy(dst[:, c0 : c0 + v, :], src[:, 0:v, :])
-                c0 += width
 
         lists = {"a": list_a, "b": list_b}
         picked = {}
@@ -102,14 +100,15 @@ def tile_moe_expert_sized_like_other_pl_kernel(
         for key in (("b", 0), ("a", 0), ("b", 1), ("a", 1)):
             picked[key] = keep.tile([P, 2, J], U32, name="picked_%s%d" % key)
 
-        def gather_plain(s, pair):
-            window = pairs[pair][:].bitcast(U32)
-            nc.vector.tensor_copy(picked[s, pair // 2][:, pair % 2, :], window.indirect(lists[s][:]))
+        def gather_plain(s, pair, j0=0, j1=J):
+            window = pairs[pair].bitcast(U32)
+            offsets = lists[s][:, j0 // 16 : j1 // 16]
+            nc.vector.tensor_copy(picked[s, pair // 2][:, pair % 2, j0:j1], window.indirect(offsets))
 
-        def weave(s, g, on_vector, m0=0, m1=P):
+        def weave(s, g, on_vector, j0=0, j1=J):
             dt = I32 if on_vector else U32
-            dst = grouped[s, g][:].bitcast(dt).rearrange("p (t m u) -> p m u t", t=4, u=2)[:, m0:m1]
-            src = picked[s, g][:].bitcast(dt).rearrange("p u (m t) -> p m u t", t=4)[:, m0:m1]
+            dst = grouped[s, g][:].bitcast(dt).rearrange("p (t a b u) -> p a t b u", t=4, b=2, u=2)[:, j0 // 8 : j1 // 8]
+            src = picked[s, g][:].bitcast(dt).rearrange("p u (a b t) -> p a t b u", t=4, b=2)[:, j0 // 8 : j1 // 8]
             if on_vector:
                 nc.vector.tensor_copy(dst, src)
             else:
@@ -152,7 +151,7 @@ def tile_moe_expert_sized_like_other_pl_kernel(
         cast(1)
         gather_plain("b", 1)
         gather_plain("a", 1)
-        weave("b", 0, False)
+        weave("b", 0, True)
         weave("a", 0, True)
         quantise("b", 0, 1)
         quantise("a", 0, 1)
@@ -160,13 +159,14 @@ def tile_moe_expert_sized_like_other_pl_kernel(
         gather_plain("b", 2)
         gather_plain("a", 2)
         cast(3)
-        gather_plain("b", 3)
-        gather_plain("a", 3)
-        weave("b", 1, False)
-        weave("a", 1, False, 0, 64)
+        wa_sb = keep.tile([P, PASSES, 2 * N], U8, name="wa_sb", tag="raw_3_2", align_bytes=64)
+        nc.sync.dma_start(wa_sb[:].bitcast(I32), wa_words.rearrange("g p n -> p g n").bitcast(I32))
+        for s in "ba":
+            for j0 in (0, J // 2):
+                gather_plain(s, 3, j0, j0 + J // 2)
+                weave(s, 1, False, j0, j0 + J // 2)
         multiply("b", 0)
         quantise("b", 1, 4)
-        weave("a", 1, True, 64, P)
         multiply("b", 1)
         quantise("a", 1, 4)
         for t in range(4):
@@ -181,7 +181,12 @@ def tile_moe_expert_sized_like_other_pl_kernel(
         factor = keep.tile([P, 4], F32, name="factor")
         part_b = keep.tile([P, 4, N], F32, name="part_b")
         y = keep.tile([P, 4, N], F32, name="y")
-        for t in range(4):
+        products = keep.tile([P, N], BF16, name="products")
+        nc.vector.tensor_scalar(part_b[:, 0, :], bank["b", 0][:], 0.3, None, ALU.mult)
+        nc.vector.scalar_tensor_tensor(
+            products[:], bank["b", 0][:], UNIT * UNIT / 0.3, part_b[:, 0, :], ALU.mult, ALU.mult, accum_out=sum_b[:, 0:1]
+        )
+        for t in range(1, 4):
             nc.scalar.activation(squares[:], bank["b", t][:], ACT.Square, scale=UNIT, accum_out=sum_b[:, t : t + 1])
             nc.vector.tensor_scalar(part_b[:, t, :], bank["b", t][:], 0.3, None, ALU.mult)
         nc.scalar.activation(denom[:], sum_b[:], ACT.Abs_reciprocal_sqrt, bias=warm[:])

@@ -18,7 +18,6 @@ ALU = mybir.AluOpType
 
 P = 128
 PASSES = 2
-UNIT = (0.01 * N) ** -0.5
 CHUNKS = ((1024, 1024), (1024, 1024), (1024, 1024), (768, 768, 512))
 VECTOR_SHARE = ((688, 688), (0, 688), (0, 256), (0, 192, 344))
 
@@ -35,9 +34,9 @@ def tile_moe_expert_sized_like_other_pl_kernel(
         list_b = keep.tile([P, J // 16], U16, name="list_b")
 
         warm = keep.tile([P, 1], F32, name="warm")
-        warm_out = keep.tile([P, 1], F32, name="warm_out")
         nc.vector.memset(warm[:], 1.0)
-        nc.scalar.activation(warm_out[:], warm[:], ACT.Abs_reciprocal_sqrt)
+        unit = keep.tile([P, 1], F32, name="unit")
+        nc.scalar.activation(unit[:], warm[:], ACT.Abs_reciprocal_sqrt, scale=0.01 * N)
 
         wa_plane = keep.tile([P, PASSES, N], U8, name="wa_plane", align_bytes=64)
         wb_plane = keep.tile([P, PASSES, N], U8, name="wb_plane", align_bytes=64)
@@ -112,7 +111,7 @@ def tile_moe_expert_sized_like_other_pl_kernel(
             if on_vector:
                 nc.vector.tensor_copy(dst, src)
             else:
-                nc.scalar.copy(dst, src)
+                nc.scalar.copy(dst.rearrange("p a t b u -> p a b t u"), src.rearrange("p a t b u -> p a b t u"))
 
         def quantise(s, g, pieces):
             w = J // pieces
@@ -183,17 +182,19 @@ def tile_moe_expert_sized_like_other_pl_kernel(
         y = keep.tile([P, 4, N], F32, name="y")
         products = keep.tile([P, N], BF16, name="products")
         nc.vector.tensor_scalar(part_b[:, 0, :], bank["b", 0][:], 0.3, None, ALU.mult)
-        nc.vector.scalar_tensor_tensor(
-            products[:], bank["b", 0][:], UNIT * UNIT / 0.3, part_b[:, 0, :], ALU.mult, ALU.mult, accum_out=sum_b[:, 0:1]
-        )
         for t in range(1, 4):
-            nc.scalar.activation(squares[:], bank["b", t][:], ACT.Square, scale=UNIT, accum_out=sum_b[:, t : t + 1])
+            nc.scalar.activation(squares[:], bank["b", t][:], ACT.Square, scale=unit[:], accum_out=sum_b[:, t : t + 1])
             nc.vector.tensor_scalar(part_b[:, t, :], bank["b", t][:], 0.3, None, ALU.mult)
+            if t == 1:
+                nc.vector.scalar_tensor_tensor(
+                    products[:], bank["b", 0][:], 1.0 / (0.3 * 0.01 * N), part_b[:, 0, :], ALU.mult, ALU.mult,
+                    accum_out=sum_b[:, 0:1],
+                )
         nc.scalar.activation(denom[:], sum_b[:], ACT.Abs_reciprocal_sqrt, bias=warm[:])
         nc.scalar.activation(recip[:], denom[:], ACT.Square)
         out_rows = out_0.rearrange("(p t) n -> p t n", t=4)
         for t in range(4):
-            nc.scalar.activation(squares[:], bank["a", t][:], ACT.Square, scale=UNIT, accum_out=sum_a[:, t : t + 1])
+            nc.scalar.activation(squares[:], bank["a", t][:], ACT.Square, scale=unit[:], accum_out=sum_a[:, t : t + 1])
             nc.scalar.activation(
                 factor[:, t : t + 1],
                 sum_a[:, t : t + 1],
@@ -214,7 +215,8 @@ def tile_moe_expert_sized_like_other_pl_kernel(
         src = y[:].rearrange("p t (c i) -> p c t i", i=4)
         split = 320 // 4
         nc.scalar.activation(dst[:, split:], src[:, split:], ACT.Copy)
-        nc.vector.tensor_copy(dst[:, :split], src[:, :split])
+        nc.vector.tensor_copy(dst[:, : half // 4], src[:, : half // 4])
+        nc.vector.tensor_copy(dst[:, half // 4 : split], src[:, half // 4 : split])
         words_out = out_1[0].rearrange("p n t -> p (n t)").bitcast(I32)
         for h, queue in ((0, nc.sync), (1, nc.scalar)):
             cols = slice(h * half, (h + 1) * half)

from contextlib import ExitStack

import concourse.mybir as mybir

K, T, J, N = 1024, 2048, 512, 512
FLOPS = 2 * 2 * J * K * N

F32 = mybir.dt.float32
BF16 = mybir.dt.bfloat16
I32 = mybir.dt.int32
U32 = mybir.dt.uint32
U16 = mybir.dt.uint16
U8 = mybir.dt.uint8
FP8X4 = mybir.dt.float8_e4m3fn_x4
FP4X4 = mybir.dt.float4_e2m1fn_x4
ACT = mybir.ActivationFunctionType
ALU = mybir.AluOpType

P = 128
PASSES = 2
CHUNKS = ((1024, 1024), (1024, 1024), (1024, 1024), (768, 768, 512))
VECTOR_SHARE = ((688, 688), (0, 688), (0, 256), (0, 192, 344))


def tile_moe_expert_sized_like_other_pl_kernel(
    tc, xt, wa_words, wa_scales, wb_words, wb_scales, offs, offs2, out_0, out_1, out_2
):
    nc = tc.nc
    with ExitStack() as ctx:
        keep = ctx.enter_context(tc.tile_pool(name="keep", bufs=1))
        psum = ctx.enter_context(tc.psum_pool(name="psum", bufs=1))

        list_a = keep.tile([P, J // 16], U16, name="list_a")
        list_b = keep.tile([P, J // 16], U16, name="list_b")

        warm = keep.tile([P, 1], F32, name="warm")
        nc.vector.memset(warm[:], 1.0)
        unit = keep.tile([P, 1], F32, name="unit")
        nc.scalar.activation(unit[:], warm[:], ACT.Abs_reciprocal_sqrt, scale=0.01 * N)

        wa_plane = keep.tile([P, PASSES, N], U8, name="wa_plane", align_bytes=64)
        wb_plane = keep.tile([P, PASSES, N], U8, name="wb_plane", align_bytes=64)
        nc.gpsimd.memset(wb_plane[:].bitcast(I32), 0)
        nc.gpsimd.memset(wa_plane[:].bitcast(I32), 0)

        x_rows = xt.rearrange("(g p u e) t -> g u p e t", g=PASSES, u=2, e=2)
        raw = {}

        def load_x(pair, c):
            width = CHUNKS[pair][c]
            c0 = T - sum(CHUNKS[pair][: c + 1])
            raw[pair, c] = keep.tile([P, 2, width], F32, name="raw_%d_%d" % (pair, c), tag="raw_%d_%d" % (pair, c), align_bytes=64)
            nc.sync.dma_start(raw[pair, c][:], x_rows[pair // 2, pair % 2, :, :, c0 : c0 + width])

        def load_plane(plane, scales):
            rows = scales.rearrange("g (q r) n -> r q g n", r=4)
            for r in range(4):
                nc.sync.dma_start(plane[:].bitcast(I32)[r:P:32], rows[r].bitcast(I32))

        wb_sb = [keep.tile([P, 4 * N], U8, name="wb_sb%d" % g, align_bytes=64) for g in range(PASSES)]
        load_x(0, 0)
        nc.sync.dma_start(list_a[:], offs)
        nc.sync.dma_start(list_b[:], offs2)
        load_x(0, 1)
        for pair in (1, 2):
            for c in range(2):
                load_x(pair, c)
        for c in range(3):
            load_x(3, c)
        load_plane(wb_plane, wb_scales)
        for g in range(PASSES):
            nc.sync.dma_start(wb_sb[g][:].bitcast(I32), wb_words[g].rearrange("p n t -> p (n t)").bitcast(I32))
        load_plane(wa_plane, wa_scales)

        pair_tiles = [keep.tile([P, 2 * T], BF16, name="pairs%d" % i, align_bytes=64) for i in range(4)]
        pairs = [tile[:] for tile in pair_tiles]

        def cast(pair):
            dst = pairs[pair].rearrange("p (t e) -> p t e", e=2)
            for c, width in enumerate(CHUNKS[pair]):
                c0 = T - sum(CHUNKS[pair][: c + 1])
                src = raw[pair, c][:].rearrange("p e t -> p t e")
                v = VECTOR_SHARE[pair][c]
                if v < width:
                    nc.scalar.activation(dst[:, c0 + v : c0 + width, :], src[:, v:width, :], ACT.Copy)
                if v > 0:
                    nc.vector.tensor_copy(dst[:, c0 : c0 + v, :], src[:, 0:v, :])

        lists = {"a": list_a, "b": list_b}
        picked = {}
        grouped = {}
        codes = {}
        plane = {}
        for s in "ba":
            for g in range(PASSES):
                grouped[s, g] = keep.tile([P, 4 * J], BF16, name="grouped_%s%d" % (s, g), align_bytes=64)
                codes[s, g] = keep.tile([P, J], U32, name="codes_%s%d" % (s, g), align_bytes=64)
                plane[s, g] = keep.tile([P, J], U8, name="plane_%s%d" % (s, g), align_bytes=64)
        for key in (("b", 0), ("a", 0), ("b", 1), ("a", 1)):
            picked[key] = keep.tile([P, 2, J], U32, name="picked_%s%d" % key)

        def gather_plain(s, pair, j0=0, j1=J):
            window = pairs[pair].bitcast(U32)
            offsets = lists[s][:, j0 // 16 : j1 // 16]
            nc.vector.tensor_copy(picked[s, pair // 2][:, pair % 2, j0:j1], window.indirect(offsets))

        def weave(s, g, on_vector, j0=0, j1=J):
            dt = I32 if on_vector else U32
            dst = grouped[s, g][:].bitcast(dt).rearrange("p (t a b u) -> p a t b u", t=4, b=2, u=2)[:, j0 // 8 : j1 // 8]
            src = picked[s, g][:].bitcast(dt).rearrange("p u (a b t) -> p a t b u", t=4, b=2)[:, j0 // 8 : j1 // 8]
            if on_vector:
                nc.vector.tensor_copy(dst, src)
            else:
                nc.scalar.copy(dst.rearrange("p a t b u -> p a b t u"), src.rearrange("p a t b u -> p a b t u"))

        def quantise(s, g, pieces):
            w = J // pieces
            for i in range(pieces):
                nc.vector.quantize_mx(
                    out=codes[s, g][:, i * w : (i + 1) * w].bitcast(FP8X4),
                    scales=plane[s, g][:, i * w : (i + 1) * w],
                    in_=grouped[s, g][:, 4 * i * w : 4 * (i + 1) * w],
                )

        bank = {}
        for s in "ba":
            for t in range(4):
                bank[s, t] = psum.tile([P, N], F32, name="bank_%s%d" % (s, t))

        def multiply(s, g, slices=range(4)):
            for t in slices:
                cols = slice(t * P, (t + 1) * P)
                if s == "a":
                    w, ws = wa_sb[:, g, :].bitcast(FP4X4), wa_plane[:, g, :]
                else:
                    w, ws = wb_sb[g][:].bitcast(FP8X4), wb_plane[:, g, :]
                nc.tensor.matmul_mx(
                    out=bank[s, t][:],
                    lhsT=codes[s, g][:, cols].bitcast(FP8X4),
                    lhsT_scale=plane[s, g][:, cols],
                    rhs=w,
                    rhs_scale=ws,
                    start=(g == 0),
                    stop=(g == PASSES - 1),
                )

        cast(0)
        gather_plain("b", 0)
        gather_plain("a", 0)
        cast(1)
        gather_plain("b", 1)
        gather_plain("a", 1)
        weave("b", 0, True)
        weave("a", 0, True)
        quantise("b", 0, 1)
        quantise("a", 0, 1)
        cast(2)
        gather_plain("b", 2)
        gather_plain("a", 2)
        cast(3)
        wa_sb = keep.tile([P, PASSES, 2 * N], U8, name="wa_sb", tag="raw_3_2", align_bytes=64)
        nc.sync.dma_start(wa_sb[:].bitcast(I32), wa_words.rearrange("g p n -> p g n").bitcast(I32))
        for s in "ba":
            for j0 in (0, J // 2):
                gather_plain(s, 3, j0, j0 + J // 2)
                weave(s, 1, False, j0, j0 + J // 2)
        multiply("b", 0)
        quantise("b", 1, 4)
        multiply("b", 1)
        quantise("a", 1, 4)
        for t in range(4):
            multiply("a", 0, (t,))
            multiply("a", 1, (t,))

        squares = keep.tile([P, N], BF16, name="squares")
        sum_a = keep.tile([P, 4], F32, name="sum_a")
        sum_b = keep.tile([P, 4], F32, name="sum_b")
        denom = keep.tile([P, 4], F32, name="denom")
        recip = keep.tile([P, 4], F32, name="recip")
        factor = keep.tile([P, 4], F32, name="factor")
        part_b = keep.tile([P, 4, N], F32, name="part_b")
        y = keep.tile([P, 4, N], F32, name="y")
        products = keep.tile([P, N], BF16, name="products")
        nc.vector.tensor_scalar(part_b[:, 0, :], bank["b", 0][:], 0.3, None, ALU.mult)
        for t in range(1, 4):
            nc.scalar.activation(squares[:], bank["b", t][:], ACT.Square, scale=unit[:], accum_out=sum_b[:, t : t + 1])
            nc.vector.tensor_scalar(part_b[:, t, :], bank["b", t][:], 0.3, None, ALU.mult)
            if t == 1:
                nc.vector.scalar_tensor_tensor(
                    products[:], bank["b", 0][:], 1.0 / (0.3 * 0.01 * N), part_b[:, 0, :], ALU.mult, ALU.mult,
                    accum_out=sum_b[:, 0:1],
                )
        nc.scalar.activation(denom[:], sum_b[:], ACT.Abs_reciprocal_sqrt, bias=warm[:])
        nc.scalar.activation(recip[:], denom[:], ACT.Square)
        out_rows = out_0.rearrange("(p t) n -> p t n", t=4)
        for t in range(4):
            nc.scalar.activation(squares[:], bank["a", t][:], ACT.Square, scale=unit[:], accum_out=sum_a[:, t : t + 1])
            nc.scalar.activation(
                factor[:, t : t + 1],
                sum_a[:, t : t + 1],
                ACT.Abs_reciprocal_sqrt,
                bias=recip[:, t : t + 1],
                scale=recip[:, t : t + 1],
            )
            nc.vector.scalar_tensor_tensor(
                y[:, t, :], bank["a", t][:], factor[:, t : t + 1], part_b[:, t, :], ALU.mult, ALU.add
            )
            nc.sync.dma_start(out_rows[:, t, :], y[:, t, :])

        y_grouped = keep.tile([P, 4 * N], BF16, name="y_grouped", align_bytes=64)
        y_codes = keep.tile([P, N], U32, name="y_codes", align_bytes=64)
        y_plane = keep.tile([P, N], U8, name="y_plane", align_bytes=64)
        half = N // 2
        dst = y_grouped[:].rearrange("p (c i t) -> p c t i", i=4, t=4)
        src = y[:].rearrange("p t (c i) -> p c t i", i=4)
        split = 320 // 4
        nc.scalar.activation(dst[:, split:], src[:, split:], ACT.Copy)
        nc.vector.tensor_copy(dst[:, : half // 4], src[:, : half // 4])
        nc.vector.tensor_copy(dst[:, half // 4 : split], src[:, half // 4 : split])
        words_out = out_1[0].rearrange("p n t -> p (n t)").bitcast(I32)
        for h, queue in ((0, nc.sync), (1, nc.scalar)):
            cols = slice(h * half, (h + 1) * half)
            nc.vector.quantize_mx(
                out=y_codes[:, cols].bitcast(FP8X4),
                scales=y_plane[:, cols],
                in_=y_grouped[:, 4 * h * half : 4 * (h + 1) * half],
            )
            queue.dma_start(words_out[:, cols], y_codes[:, cols].bitcast(I32))
        scale_rows = out_2[0].rearrange("(q r) n -> r q n", r=4)
        for r in range(4):
            queue = nc.sync if r % 2 == 0 else nc.scalar
            queue.dma_start(scale_rows[r].bitcast(I32), y_plane[:].bitcast(I32)[r:P:32])
